import numpy as np, ml_dtypes
CORES = [35,38,43,46]
N = 4
BF = ml_dtypes.bfloat16
W, L, RO, SH = 4096, 256, 8, (1,)
KK = np.arange(16, dtype=np.int32).reshape(1, 1, 16, 1)
REC = np.array([0.3, 0.0, 1.0, 0.5, 1.0, 0.3, 1.0, 1.0]).reshape(1, 8, 1, 1)
def spans(rng, kind):
    p = np.argsort(rng.random((N, 8, 16, L)), axis=2).astype(np.float64); x = rng.random((N, 8, 16, L)); t = rng.random((N, 8, 16, L))
    s = np.exp2(-rng.integers(0, 6, (N, 8, 1, L)).astype(np.float64))
    c = np.where((kind == 1) | (kind == 3), p, x)
    dur = np.where(kind == 1, 0.5, np.where(kind == 2, 1.0 + t, np.where(kind == 3, 31.0 - 2.0 * p, t * s)))
    pos = np.argsort(np.argsort(np.concatenate([c, c + dur], axis=2), axis=2, kind="stable"), axis=2)
    return pos[:, :, :16], pos[:, :, 16:]
def kinds(rng):
    return rng.choice(np.array([0, 0, 0, 0, 1, 2, 3]), (N, 8, 1, L))
def parts(rng):
    xt = np.floor(rng.random((N, 8, 16, W)) * rng.choice(np.array([12, 24, 40, 64]), (N, 8, 1, W))).astype(np.int64)
    vt = rng.integers(0, 64, (N, 8, 16, W))
    z0 = np.floor(rng.random((N, 8, 16, L)) * rng.choice(np.array([16, 32, 64]), (N, 8, 1, L))).astype(np.int64)
    nm = rng.integers(0, 4096, (N, 8, 16, L)); wt = rng.integers(0, 4096, (N, 8, 16))
    th = rng.integers(150, 330, (N, 8, 1)) + rng.integers(-60, 61, (N, 8, 16))
    th[np.arange(N), rng.integers(0, 8, N)] = rng.integers(0, 30, (N, 16))
    return xt, vt, z0, nm, wt, th
def aim(c):
    return (c - 37 * KK) & 4095
def few(a):
    return np.ascontiguousarray(np.reshape(a, (N, 128, -1))).astype(np.float32).astype(BF)
def big(a):
    return np.ascontiguousarray(np.reshape(a, (N, 128, -1))).astype(np.int32)
def pack(xt, vt, z0, nm, ca, rt, wt, th):
    return {"xt": few(xt), "vt": few(vt), "z0": few(z0), "nm": big(nm), "ca": few(ca), "rt": few(rt), "wt": big(wt), "th": big(th)}
def setup_inputs(rng):
    xt, vt, z0, nm, wt, th = parts(rng); ca, rt = spans(rng, kinds(rng))
    return pack(xt, vt, z0, nm, ca, rt, wt, th)
def uneven(rng, bits, *shape):
    return np.minimum(np.floor(np.exp2(bits * rng.random(shape))), 2 ** bits).astype(np.int64) - 1
def sized(rng, n):
    a = np.minimum(np.floor(np.exp2(6.0 * rng.random((N, 8, 1, n))) * rng.random((N, 8, 16, n))), 63).astype(np.int64)
    return np.where(rng.random((N, 8, 1, n)) < 0.5, a, 63 - a)
def setup_inputs_spread(rng):
    ca, rt = spans(rng, kinds(rng))
    return pack(sized(rng, W), sized(rng, W), sized(rng, L), uneven(rng, 12, N, 8, 16, L), ca, rt, uneven(rng, 12, N, 8, 16), np.minimum(uneven(rng, 10, N, 8, 16), 1007))
def tips(rng, n):
    return np.where(rng.random((N, 8, 1, n)) < REC, 63 * rng.integers(0, 2, (N, 8, 1, n)), 63 * rng.integers(0, 2, (N, 8, 16, n)))
def setup_inputs_ends(rng):
    xt, vt, z0 = tips(rng, W), tips(rng, W), tips(rng, L)
    nm = 4095 * rng.integers(0, 2, (N, 8, 16, L)); wt = 4095 * rng.integers(0, 2, (N, 8, 16)); th = 1007 * rng.integers(0, 2, (N, 8, 16))
    th[:, :, 0] = 0; th[:, :, 15] = 1007
    us = np.arange(W); hit = np.flatnonzero((((us * us) >> 5) + 37 * us + 613) & (W - 1) == W - 1)
    one = 65 if len(hit) == 0 else (-65 * int(hit[rng.integers(0, len(hit))])) & 4095
    wt[:, 0] = 4095; wt[:, 6:] = 0; wt[:, 7, 15] = 65; wt[:, 6, 15] = one
    last = np.array([0, 1, 6, L - 2, L - 1])
    z0[:, 0][..., last] = 63; z0[:, 7][..., last] = 63; nm[:, 7][..., last] = 4095
    ca, rt = spans(rng, rng.choice(np.array([1, 2, 3]), (N, 8, 1, L)))
    return pack(xt, vt, z0, nm, ca, rt, wt, th)
def setup_inputs_corners(rng):
    xt, vt, z0, nm, wt, th = parts(rng); H = W // 2
    hi = rng.integers(0, 64, (N, 4, 16, H)) * (rng.random((N, 4, 1, H)) < 0.5); hi[:, :, :8] = 63; hi[:, :, 8] = 0
    lo = np.where(rng.random((N, 4, 1, H)) < 0.5, 63, rng.integers(0, 64, (N, 4, 16, H))); lo[:, :, :9] = 0
    xt[:, :4, :, :H] = hi; xt[:, :4, :, H:] = lo; z0[:, :4] = rng.integers(1, 63, (N, 4, 16, L)); wt[:, :4] = 0; th[:, :4] = 0
    kind = kinds(rng); kind[:, :4] = rng.choice(np.array([1, 2, 2, 3]), (N, 4, 1, L)); kind[:, 4] = 1; kind[:, 5] = 2; kind[:, 6] = 3
    ca, rt = spans(rng, kind)
    many = rng.choice(np.array([0, 1, RO // 2, RO - 2, RO - 1, 16]), (N, 8, 1, L)); many[:, 1] = rng.integers(0, 2, (N, 1, L)); many[:, 2] = RO // 2; many[:, 3] = 16
    many[:, 0, :, L - 1] = RO - 2
    order = np.argsort(np.argsort(ca, axis=2), axis=2)
    c = np.where(order < many, rng.integers(0, H - 32, (N, 8, 16, L)), rng.integers(H, W - 32, (N, 8, 16, L)))
    nm[:, :4] = aim(c)[:, :4]
    wt[:, 4] = 4095 * rng.integers(0, 2, (N, 16)); th[:, 4] = 0; th[:, 7] = np.where(rng.random((N, 16)) < 0.25, 1007, 0)
    return pack(xt, vt, z0, nm, ca, rt, wt, th)
def setup_inputs_crowd(rng):
    xt, vt, z0, nm, wt, th = parts(rng); Q = W // 4
    xt[..., :Q] = rng.integers(40, 64, (N, 8, 16, Q)); xt[..., Q:2 * Q] = rng.integers(24, 33, (N, 8, 16, Q)); xt[..., 2 * Q:] = 0
    z0 = rng.integers(1, 8, (N, 8, 16, L)); wt[:, 0::2] = 0; wt[:, 1::2] = W // 2
    xt[:, 1::2] = (xt[:, 1::2] >> 1) << 1; z0[:, 1::2] = np.maximum((z0[:, 1::2] >> 1) << 1, 2)
    vt[..., 613] = 0; th = rng.integers(0, 300, (N, 8, 16))
    ca, rt = spans(rng, kinds(rng)); first = ca == np.min(ca, axis=2, keepdims=True)
    low = rng.integers(2 * Q, W - 32, (N, 8, 16, L)); mid = rng.integers(Q, 2 * Q - 32, (N, 8, 16, L))
    c = np.where(first, rng.integers(0, Q - 32, (N, 8, 16, L)), np.where(rng.random((N, 8, 1, L)) < 0.5, mid, low))
    out = np.zeros((N, 8, 1, L), bool); out[1, 7, 0, L - 1] = True
    for q in range(2, N - 1):
        for g in range(1, 8, 2): out[q, g, 0, rng.integers(0, L)] = True
    nm = aim(np.where(out, low, c))
    e = N - 1; cols = np.arange(W)
    xt[e] = rng.integers(0, 64, (8, 16, W)); xt[e, :, 8:] = xt[e, :, 8:] >> 2; vt[e, :, 8:] = vt[e, :, 8:] >> 2
    z0[e, :, :8] = 0; z0[e, :, 8:] = rng.integers(50, 64, (8, 8, L)); th[e] = rng.integers(0, 100, (8, 16))
    wt[e, 0::2] = rng.integers(0, 4096, (4, 16)); nm[e, 0::2] = rng.integers(0, 4096, (4, 16, L))
    wt[e, 1::2] = 0; wt[e, 1::2, 0] = 1; wt[e, 1::2, 1] = 64
    xt[e, 1::2, 0] = cols & 63; xt[e, 1::2, 1] = cols >> 6; xt[e, 1::2, 2] = np.where(cols < 600, 0, rng.integers(1, 64, (4, W)))
    us = np.arange(600, W); us = us[np.unique(((us * us >> 5) + 37 * us) & (W - 1), return_index=True)[1]]
    for g in range(1, 8, 2): nm[e, g] = np.where(first[e, g], aim(np.resize(rng.permutation(us), L))[0, 0], 0)
    return pack(xt, vt, z0, nm, ca, rt, wt, th)
def setup_inputs_twins(rng):
    xt, vt, z0, nm, wt, th = parts(rng); B = W // 128
    b = np.floor(rng.random((1, 8, 16, B)) * rng.choice(np.array([12, 24, 40, 64]), (1, 8, 1, B))).astype(np.int64)
    xt = np.repeat(np.repeat(b, 128, axis=3), N, axis=0)
    a = rng.integers(0, 40, (1, 8, 16, L // 2)); z0 = np.repeat(np.concatenate([a, a], axis=3), N, axis=0)
    a = rng.integers(0, 4096, (1, 8, 16, L // 2)); nm = np.repeat(np.concatenate([a, a], axis=3), N, axis=0)
    wt = np.repeat(wt[:1], N, axis=0); th = rng.integers(0, 4, (N, 8, 16)); ca, rt = spans(rng, kinds(rng))
    return pack(xt, vt, z0, nm, ca, rt, wt, th)
def check_inputs(d):
    bad = []
    for k, lo, hi in (("xt", 0, 63), ("vt", 0, 63), ("z0", 0, 63), ("nm", 0, 4095), ("ca", 0, 30), ("rt", 1, 31), ("wt", 0, 4095), ("th", 0, 1007)):
        a = np.asarray(d[k]).astype(np.float64)
        if not np.all((a >= lo) & (a <= hi)): bad.append("range of " + k)
        elif not np.all(a == np.floor(a)): bad.append("whole numbers in " + k)
    c = np.asarray(d["ca"]).astype(np.float64).reshape(N, 8, 16, L); r = np.asarray(d["rt"]).astype(np.float64).reshape(N, 8, 16, L)
    if not np.all(c < r): bad.append("ca under rt")
    e = np.sort(np.concatenate([c, r], axis=2), axis=2)
    if not np.all(e[:, :, 1:] > e[:, :, :-1]): bad.append("positions of a lane distinct")
    return bad
def ints(a):
    return np.asarray(a).astype(np.float32).astype(np.int32)
def pick(t, ix):
    return np.stack([np.stack([np.take(t[q, g], ix[q, g], axis=1) for g in range(8)]) for q in range(N)])
def mark(x, w):
    return np.sum(x * w, axis=2, dtype=np.int32) & (W - 1)
def place(u, d):
    return ((u * u >> 5) + 37 * u + 613 * d) & (W - 1)
def reference(xt, vt, z0, nm, ca, rt, wt, th):
    X = ints(xt).reshape(N, 8, 16, W); V = ints(vt).reshape(N, 8, 16, W); z = ints(z0).reshape(N, 8, 16, L)
    n = nm.astype(np.int32).reshape(N, 8, 16, L); c = ints(ca).reshape(N, 8, 16, L); r = ints(rt).reshape(N, 8, 16, L)
    w = wt.astype(np.int32).reshape(N, 8, 16, 1); t = th.astype(np.int32).reshape(N, 8, 16, 1)
    lev = np.zeros((N, 8, 16, L), np.int32); dep = np.zeros((N, 8, L), np.int32); ptr = np.full((N, 8, L), -1, np.int32)
    stk = np.zeros((N, 8, 16, RO, L), np.int32); A = np.zeros((N, 1, 1, 1), np.int32); height = np.arange(RO).reshape(1, 1, 1, RO, 1)
    for step in range(RO):
        kap = np.min(np.where(lev > 0, 32, r), axis=2, keepdims=True)
        can = (lev == 0) & (c > ptr[:, :, None]) & (c < kap)
        uz = mark(z, w); zz = z[:, :, :, None]
        y = pick(X, ((n * uz[:, :, None] >> 5) + n + 37 * KK + A) & (W - 1))
        zk = np.abs(zz - y); rows = np.sum(y >= zz, axis=2, dtype=np.int32)
        v = pick(V, place(mark(zk, w[..., None]), dep[:, :, None] + 1))
        far = np.sum(np.abs(v - zk), axis=2, dtype=np.int32)
        key = np.where(can & (rows >= 8) & (far > t), c, 32)
        k = np.argmin(key, axis=2); push = np.min(key, axis=2) < 32; pop = ~push & (dep > 0)
        at = place(uz, dep); wins = {}
        for q in range(N):
            for g in range(8):
                i = np.flatnonzero(pop[q, g]); p, f = np.unique(at[q, g, i], return_index=True)
                wins[q, g] = (p, z[q, g][:, i[f]])
        for d in (0,) + SH:
            for q in range(N):
                for g in range(8):
                    V[(q + d) % N, g][:, wins[q, g][0]] = wins[q, g][1]
        old = np.take_along_axis(stk, np.maximum(dep - 1, 0)[:, :, None, None, :], axis=3)[:, :, :, 0]
        new = np.take_along_axis(zk, k[:, :, None, None, :], axis=3)[:, :, :, 0]
        stk = np.where(push[:, :, None, None, :] & (dep[:, :, None, None, :] == height), zz, stk)
        P, O, D = push[:, :, None], pop[:, :, None], dep[:, :, None]
        top = O & (lev == D)
        ptr = np.where(pop, np.sum(np.where(top, c, 0), axis=2, dtype=np.int32), -1)
        lev = np.where(P & (KK == k[:, :, None]), D + 1, np.where(top, 0, lev))
        z = np.where(P, new, np.where(O, old, 63 - z))
        dep = dep + push.astype(np.int32) - pop.astype(np.int32)
        A = (np.sum(pop, axis=(1, 2)) & 31).reshape(N, 1, 1, 1)
    return {"yv": V.reshape(N, 128, W).astype(np.float32).astype(BF), "yz": z.reshape(N, 128, L).astype(np.float32).astype(BF),
            "yl": lev.reshape(N, 128, L).astype(np.float32).astype(BF), "yp": ptr.astype(np.float32)}

from concourse.mybir import AluOpType as Op, AxisListType, ActivationFunctionType as Act

STEPS = 8
NE = 9
FL, ZS = 4096, 4352
LAT, CYC, GAT, WIN = 0.1, 0.00083, 1.56, 0.02
BIAS = {"x": -3.6, "gx": -3, "ln": -1.4, "sc": -0.9, "pk": -16.5, "bb": -0.1, "row": -12.0, "mv": -0.8, "ab": 4.2, "far": 7.8,
        "vi": 1.6, "dd": 1.9, "vg": -2.2, "sh": -3.4}
_B = {
    "bfloat16": "XT 4128 VT 4352 ZW 6656 D 4096 BB 4096 EE 4096 AB 4096 CMP 4096 ZIN 2048 CAI 256 RTI 256 CAT 256 RTT 256 CAC 256 CAB 256 "
                "RTB 256 CM 256 G1 256 HIT 256 LEV0 256 LEV1 256 HD 144 RED 2048 BSEL 2048 TRI 2048 ONE 2048 ZER 256 BLK 128 IDN 128 NEG 128 "
                "I64 128 N64 128 I1K 128 I32 128 PAR 128 NPAR 128 SM 512 UPQ 256 OFFD 256 LEV 256 YLB 256 LB 2048 Z4 1024",
    "float16": "PR 256 NMF 256 NMT 256 THM 256 WRED 2048 D19 128 LH 64",
    "uint16": "WIN 128 WO 128 XO 256 HO 256 ZO 32",
    "int32": "NMI 256 WTI 1 THI 1 NB 256 NK 256 K37 256 T2 256 T3 256 V1 256 UM 256 V3 256 V4 256 V5 256 LI 4096",
    "float32": "KC 256 TH 256 PK 256 KEY 64 RM 256 KS 256 CS 256 HC 144 DC 144 TS 144 RS9 144 RSA 256 RSM 256 IO3 256 IO4 256 IO5 144 "
               "LVT 256 YL 256 YP 256 LF 2048",
}
SCRATCH = {}
for _t in _B:
    _w = _B[_t].split()
    for _i in range(0, len(_w), 2):
        SCRATCH[_w[_i]] = ("sbuf", [128, int(_w[_i + 1])], _t)
for _i in range(8):
    SCRATCH["pb%d" % _i] = ("psum", [128, 512], "float32")
LOADS = ["lnm", "lwt", "lca", "lx", "lxw", "lz", "lrt", "lth", "lv"]
OUTS = ["ov", "oz", "ol", "op"]
SEMAPHORES = ["sv", "ss", "st", "sg", "loc"] + LOADS + OUTS + ["az%d" % s for s in range(1, STEPS)] + ["aw%d" % s for s in range(1, STEPS)]
QSEM = {"vector": "sv", "scalar": "ss", "tensor": "st", "gpsimd": "sg"}
SIZE = {"bfloat16": 2, "float16": 2, "uint16": 2, "float32": 4, "int32": 4}


def rank_program(g, core, T, topo):
    rank = T.rank_of(core)
    if rank is None:
        return
    n = len(T.cores)
    nxt, prv = T.cores[(rank + 1) % n], T.cores[(rank - 1) % n]
    ops = []
    tag = ["init"]
    slots, used = {}, {"LF": 0, "LI": 0, "LB": 0, "LH": 0}

    def v(name, c0=0, c1=None, st=1):
        return (name, c0, SCRATCH[name][1][1] if c1 is None else c1, st)

    def ap(x):
        return T[x[0]][:, x[1]:x[2]] if x[3] == 1 else T[x[0]][:, x[1]:x[2]:x[3]]

    def width(x):
        return (x[2] - x[1] + x[3] - 1) // x[3]

    def psum(x):
        return SCRATCH[x[0]][0] == "psum"

    def size(x):
        return SIZE[SCRATCH[x[0]][2]]

    def sub(x, a, b):
        return (x[0], x[1] + a, x[1] + b, 1)

    def h16(x):
        return sub(x, 0, 16)

    def lane(name, buf, w=32):
        if name not in slots:
            slots[name] = v(buf, used[buf], used[buf] + w)
            used[buf] += w
        return slots[name]

    def add(q, fn, rd, wr, cost, done=None, pre=()):
        ops.append({"q": q, "fn": fn, "rd": list(rd), "wr": list(wr), "cost": cost, "done": done, "pre": list(pre), "tag": tag[0]})

    def vcost(cyc):
        return max(64, cyc) * CYC

    def half(a, b):
        return 0.5 if size(a) == 2 and size(b) == 2 else 1

    def tt(out, a, b, op):
        add("vector", lambda: [g.vector.tensor_tensor(ap(out), ap(a), ap(b), op)], [a, b], [out],
            vcost(width(out) * (1 if psum(a) or psum(b) else 2)))

    def ts(out, a, s1, op0, s2=None, op1=None):
        def val(s):
            return ap(s) if isinstance(s, tuple) else s

        def fn():
            if op1 is None:
                return [g.vector.tensor_scalar(ap(out), ap(a), val(s1), None, op0)]
            return [g.vector.tensor_scalar(ap(out), ap(a), val(s1), val(s2), op0, op1)]
        add("vector", fn, [a] + [s for s in (s1, s2) if isinstance(s, tuple)], [out], vcost(width(out) * half(out, a)))

    def cp(out, a):
        add("vector", lambda: [g.vector.tensor_copy(ap(out), ap(a))], [a], [out], vcost(width(out) * half(out, a)))

    def fill(out, c):
        add("vector", lambda: [g.vector.memset(ap(out), c)], [], [out], vcost(width(out) * half(out, out)))

    def scan(out, d0, d1, op0, op1):
        add("vector", lambda: [g.vector.tensor_tensor_scan(ap(out), ap(d0), ap(d1), 0.0, op0, op1)], [d0, d1], [out], vcost(width(out)))

    def turn(out, a):
        add("vector", lambda: [g.vector.transpose(ap(out), ap(a))], [a], [out], vcost(width(out)))

    def act(out, a, func, scale=1.0, bias=0.0):
        add("scalar", lambda: [g.scalar.activation(ap(out), ap(a), func, bias=bias, scale=scale)], [a], [out], max(64, width(out)) * CYC)

    def mms(lst):
        rd, wr, c = [], [], 0
        for o, l, r, a, b in lst:
            rd += [l, r]
            wr.append(o)
            c += max(64, width(r))
        add("tensor", lambda: [g.tensor.matmul(ap(o), ap(l), ap(r), a, b) for o, l, r, a, b in lst], rd, wr, c * CYC)

    def iota(out, pattern, base, cm):
        if SCRATCH[out[0]][2] == "int32":
            fn = lambda: [g.iota(ap(out), pattern, base, cm)]
        else:
            fn = lambda: [g.iota(ap(out), pattern, base, cm, allow_small_or_imprecise_dtypes=True)]
        add("gpsimd", fn, [], [out], 0.13 + 2 * width(out) * CYC)

    def asel(out, a, pattern, cmp, base, cm):
        add("gpsimd", lambda: [g.affine_select(ap(out), ap(a), pattern, cmp, 0.0, base, cm)], [a], [out], 0.17 + 2 * width(out) * CYC)

    def dma(q, out, src, rd, wr, sem, cost):
        eng = g.sync if q == "sync" else g.scalar
        add(q, lambda: [eng.dma_start(out, src)], rd, wr, cost, done=(sem, 16))

    dma("scalar", T.NMI[:], T.nm[:], [], [v("NMI")], "lnm", 2.5)
    dma("scalar", T.ZW[:, ZS:ZS + 256], T.z0[:], [], [v("ZW", ZS, ZS + 256)], "lz", 2.5)
    dma("sync", T.WTI[:], T.wt[:], [], [v("WTI")], "lwt", 2.5)
    dma("scalar", T.THI[:], T.th[:], [], [v("THI")], "lth", 2.5)
    dma("sync", T.CAI[:], T.ca[:], [], [v("CAI")], "lca", 2.5)
    dma("scalar", T.RTI[:], T.rt[:], [], [v("RTI")], "lrt", 2.5)
    dma("sync", T.XT[:, 0:4096], T.xt[:], [], [v("XT", 0, 4096)], "lx", 8.0)
    dma("scalar", T.XT[:, 4096:4128], T.xt[:, 0:32], [], [v("XT", 4096, 4128)], "lxw", 3.0)
    dma("sync", T.VT[:, 0:4096], T.vt[:], [], [v("VT", 0, 4096)], "lv", 12.0)

    one = v("ONE", 0, 128)
    fill(v("ONE"), 1.0)
    fill(v("ZER"), 0.0)
    fill(v("RED"), 0.0)
    gv, ga, gb, gB = lane("gv", "LF", 8), lane("ga", "LF", 8), lane("gb", "LF", 8), lane("gB", "LF", 8)
    pI, lI = lane("pI", "LI", 16), lane("lI", "LI", 16)
    iota(gv, [[-16, 8]], 0, 1)
    iota(pI, [[0, 16]], 0, 1)
    iota(lI, [[16, 16]], 0, 0)
    asel(v("IDN"), one, [[-1, 128]], Op.is_equal, 0, 1)
    asel(v("UPQ", 0, 128), one, [[-1, 128]], Op.is_equal, -16, 1)
    asel(v("UPQ", 128, 256), one, [[-1, 128]], Op.is_equal, 16, 1)
    iota(v("PAR"), [[0, 4], [1, 2], [0, 16]], 0, 0)
    iota(v("K37"), [[37, 16], [0, 16]], 0, 0)
    iota(v("IO3"), [[0, 16], [1, 16]], 0, 0)
    iota(v("IO4"), [[1, 16], [0, 16]], 0, 0)
    asel(v("BLK"), one, [[-16, 8], [0, 16]], Op.is_ge, 0, 1)
    asel(v("BLK"), v("BLK"), [[16, 8], [0, 16]], Op.is_ge, 15, -1)
    iota(v("KC"), [[4096, 16], [0, 16]], 32 * 131072, 0)
    iota(v("IO5"), [[0, 16], [1, NE]], 0, 0)
    ts(v("NPAR"), v("PAR"), -1.0, Op.mult, 1.0, Op.add)

    def smx(gp, lhp):
        return v("SM", 128 * (2 * gp + lhp), 128 * (2 * gp + lhp) + 128)
    for gp in range(2):
        for lhp in range(2):
            src = v("IDN") if gp == lhp else v("UPQ", 0, 128) if lhp == 1 else v("UPQ", 128, 256)
            tt(smx(gp, lhp), src, v("PAR") if gp else v("NPAR"), Op.mult)
    ts(ga, gv, 0.0, Op.is_ge)
    ts(gb, gv, 15.0, Op.is_le)
    tt(gB, ga, gb, Op.mult)
    for lp in range(16):
        cp(v("RED", lp * 128 + lp, lp * 128 + 128, 16), gB)
    wh, wf = lane("wh", "LF", 1), lane("wf", "LF", 1)
    ts(wh, v("WTI"), 2048.0, Op.is_ge, -4096.0, Op.mult)
    tt(wf, wh, v("WTI"), Op.add)
    ts(v("WRED"), v("RED"), wf, Op.mult)
    for nm, c in (("NEG", -1.0), ("I64", 64.0), ("N64", -64.0), ("I1K", 1024.0), ("I32", 32.0), ("D19", 19616.0)):
        ts(v(nm), v("IDN"), c, Op.mult)

    def mat(name, lp):
        return v(name, lp * 128, lp * 128 + 128)
    u0, uI, u4 = v("pb1", 256, 272), lane("uI", "LI", 64), lane("u_0", "LI", 64)
    mms([(u0, mat("WRED", lp), v("ZW", ZS + lp, ZS + 256, 16), lp == 0, lp == 15) for lp in range(16)])
    for q in range(4):
        cp(sub(uI, 16 * q, 16 * q + 16), u0)
    ts(u4, uI, 4095, Op.bitwise_and)

    def conv_k(bank, c0, src):
        mms([(v(bank, c0 + k * 16 + lhp, c0 + k * 16 + 16, 2), smx(gp, lhp), v(src, gp * 16 + k, 256, 32), gp == 0, gp == 1)
             for k in range(16) for lhp in range(2) for gp in range(2)])
    ts(v("NMF"), v("NMI"), -2048.0, Op.add)
    turn(v("NMT"), v("NMF"))
    conv_k("pb6", 0, "NMT")
    ts(v("NB"), v("pb6", 0, 256), 2048.0, Op.add)
    tt(v("T3"), v("NB"), v("K37"), Op.add)
    ts(v("T2"), v("T3"), 4095, Op.bitwise_and)
    ts(v("NK"), v("T2"), 32.0, Op.mult, -131072.0, Op.add)
    turn(v("CAT"), v("CAI"))
    turn(v("RTT"), v("RTI"))
    conv_k("pb0", 256, "CAT")
    mms([(v("pb0", (2 * b + lhp) * 16, (2 * b + lhp) * 16 + 16), smx(gp, lhp), v("RTT", 32 * b + 16 * gp, 32 * b + 16 * gp + 16), gp == 0, gp == 1)
         for b in range(8) for lhp in range(2) for gp in range(2)])
    RTP, CAN = v("pb0", 0, 256), v("pb0", 256, 512)
    CB = v("pb7", 0, 256)
    ts(v("CAC"), CAN, -1.0, Op.mult, 32.0, Op.add)
    ts(v("KS"), CAN, -131072.0, Op.mult)
    tt(CB, v("KS"), v("KC"), Op.add)
    cp(v("RTB"), RTP)
    cp(v("CAB"), CAN)
    fill(v("LEV0"), 0.0)
    pm, lc, dmp = lane("pm", "LI", 16), lane("lc", "LI", 16), lane("dmp", "LF", 16)
    pf, thf = lane("pf", "LF", 1), lane("thf", "LF", 1)
    ts(pm, pI, 15, Op.bitwise_and)
    tt(lc, pm, lI, Op.add)
    ts(dmp, lc, 4096.0, Op.add)
    cp(pf, sub(pm, 0, 1))
    cp(thf, v("THI"))
    ts(v("THM"), v("IO4"), pf, Op.is_equal, thf, Op.mult)
    mms([(v("pb4", 256, 512), v("BLK"), v("THM"), True, True)])
    ts(v("TH"), v("pb4", 256, 512), 1024.0, Op.add)
    ts(v("OFFD"), v("IO3"), pf, Op.not_equal, -1000.0, Op.mult)
    ts(v("RSM"), v("IO3"), 0.0, Op.is_gt)
    ts(v("RSA"), v("RSM"), -1001.0, Op.mult, 1000.0, Op.add)
    ts(v("RS9"), v("IO5"), 0.0, Op.is_gt)
    wq, si, si2, s63 = lane("wq", "LH", 2), lane("si", "LI", 1), lane("si2", "LI", 1), lane("s63", "LF", 1)
    cp(sub(wq, 0, 1), wf)
    mms([(v("pb1", 280, 281), v("BLK"), sub(wq, 0, 1), True, True)])
    ts(si, v("pb1", 280, 281), 63.0, Op.mult)
    ts(si2, si, 4095, Op.bitwise_and)
    cp(s63, si2)
    asel(v("BSEL"), v("ONE"), [[-1, 16], [-16, 8], [0, 16]], Op.is_equal, 0, 1)
    asel(v("TRI"), v("ONE"), [[0, 16], [-16, 8], [0, 16]], Op.is_ge, 0, 1)
    asel(v("TRI"), v("TRI"), [[1, 16], [16, 8], [0, 16]], Op.is_ge, -1, -1)
    fill(lane("d_0", "LB"), 0.0)
    fill(lane("ptr_0", "LB"), 0.0)
    fill(v("HD"), -1.0)
    fill(v("HD", 0, 144, NE), 0.0)
    fill(v("HC"), 0.0)
    A = None

    for s in range(STEPS):
        par, nxp, last = "_%d" % (s % 2), "_%d" % ((s + 1) % 2), s == STEPS - 1

        def L(name, buf, w=32, par=par):
            return lane(name + par, buf, w)
        u, d = L("u", "LI", 64), L("d", "LB")
        z = v("ZW", ZS + 256 * s, ZS + 256 * s + 256)
        if s:
            en = topo.engines(core, nxt)[:8]
            rid, pid = topo.addr(nxt)[:2]

            def send(dst, src, sem, mask=sum(1 << e for e in en), rid=rid, pid=pid):
                def fn():
                    g.remote_dma(out_ap=ap(dst), in_ap=ap(src), remote_sem=T.sem[sem], local_sem=T.sem.loc, pid=pid, routing_id=rid, dma_engine_mask=mask)
                    return []
                add("gpsimd", fn, [src], [], 1.0, done=("none", 0))
            zin, win, wo = v("ZIN", 256 * s, 256 * s + 256), v("WIN", 16 * s, 16 * s + 16), v("WO", 16 * s, 16 * s + 16)
            send(zin, z, "az%d" % s)
        tag[0] = "x"
        for q in range(4):
            c0, c1 = 64 * q, 64 * q + 64
            t1, t2, t3, xo = v("pb7", 256 + c0, 256 + c1), v("T2", c0, c1), v("T3", c0, c1), v("XO", c0, c1)
            tt(t1, v("NB", c0, c1), u, Op.mult)
            tt(t2, t1, v("NK", c0, c1), Op.add)
            ts(t3, t2, 5, Op.arith_shift_right, 4095, Op.bitwise_and)
            if A is None:
                cp(xo, t3)
            else:
                ts(xo, t3, A, Op.add)
        tag[0] = "sh"
        d1, d2 = L("d1", "LB", 64), L("d2", "LB")
        act(sub(d1, 0, 32), d, Act.Identity, bias=1.0)
        act(sub(d1, 32, 64), d, Act.Identity, bias=1.0)
        act(d2, d, Act.Identity, scale=2.0, bias=1.0)
        DR, dr = v("pb2", 0, 256), v("pb2", 256, 400)
        mms([(sub(DR, 64 * i, 64 * i + 64), v("D19"), d1, True, True) for i in range(4)])
        fa, fb = L("fa", "LI", 16), L("fb", "LI", 16)
        ts(fa, h16(u), -1.0, Op.mult, s63, Op.add)
        ts(fb, fa, 4095, Op.bitwise_and)
        cp(v("HC", 0, 144, NE), fb)
        mms([(v("pb2", 256 + e, 400, NE), v("IDN"), h16(d), True, True) for e in range(s + 1 if s else NE)])
        tt(dr, v("HD"), dr, Op.is_equal)
        tt(v("DC"), dr, v("HC"), Op.mult)
        scan(v("TS"), v("RS9"), v("DC"), Op.mult, Op.max)
        top, ta, tb, tc, tca, pt = L("top", "LI"), L("ta", "LI"), L("tb", "LI"), L("tc", "LI"), L("tca", "LI"), L("pt", "LB")
        cp(sub(top, 0, 16), v("TS", NE - 1, 144, NE))
        cp(sub(top, 16, 32), v("TS", NE - 1, 144, NE))
        ts(ta, top, 4095, Op.bitwise_and)
        ts(tb, top, 6, Op.arith_shift_right, 0xF000, Op.bitwise_and)
        tt(tc, ta, tb, Op.add)
        ts(tca, top, 12, Op.arith_shift_right, 63, Op.bitwise_and)
        ts(pt, tca, -1.0, Op.mult, 33.0, Op.add)
        scan(v("KS"), v("RSA"), RTP, Op.max, Op.min)
        act(v("CM"), CAN, Act.Sign, bias=0.5)
        kk, kth, kp, dp, alt = L("kk", "LF"), L("kth", "LF"), L("kp", "LF"), L("dp", "LF"), L("alt", "LF")
        for i in range(2):
            act(sub(kk, 16 * i, 16 * i + 16), v("KS", 15, 256, 16), Act.Identity, scale=-131072.0, bias=32.0 * 131072 + 65536)
        act(kth, kk, Act.Identity, bias=65536.0)
        act(dp, d, Act.Sign)
        tt(kp, kth, dp, Op.mult)
        tt(alt, tc, kk, Op.add)
        act(v("ZW", FL, FL + 256), z, Act.Identity, scale=-1.0, bias=63.0)
        tag[0] = "pl"
        if s:
            pa, pb, pc, pd, pe = L("pa", "LI", 16), L("pb", "LI", 16), L("pc", "LF", 16), L("pd", "LI", 16), L("pe", "LI", 16)
            ps, ad = L("ps", "LH", 16), L("ad", "LF", 16)
            ts(pa, h16(u), 1184.0, Op.add)
            tt(pb, pa, h16(u), Op.mult)
            act(pc, h16(d), Act.Copy, scale=19616.0)
            tt(pd, pb, pc, Op.add)
            ts(pe, pd, 5, Op.arith_shift_right, 4095, Op.bitwise_and)
            ts(ps, pe, -2048.0, Op.add)
            tt(ad, pe, dmp, Op.subtract)
            mms([(v("pb6", lp, 256, 16), mat("BSEL", lp), ps, True, True) for lp in range(16)])
            cp(v("PR"), v("pb6", 0, 256))
        for q in range(4):
            a, b, c0, c1 = 1024 * q, 1024 * q + 1024, 64 * q, 64 * q + 64
            tag[0] = "gx"
            if q:
                def gx4(a=a, b=b, c0=c0, c1=c1):
                    return [g.vector.tensor_tensor(T.D[:, a:b], T.XT[:, 0:4128].indirect(T.XO[:, c0:c1]), T.Z4[:], Op.subtract)]
                add("vector", gx4, [v("XT"), v("XO", c0, c1), v("Z4")], [v("D", a, b)], 0.05 + GAT * 1024 * CYC)
            else:
                act(v("Z4", 0, 256), z, Act.Copy)
                act(v("Z4", 256, 512), z, Act.Copy)
                act(v("Z4", 512, 1024), v("Z4", 0, 512), Act.Copy)
                for k in range(4):
                    def gx(k=k, z=z):
                        return [g.vector.tensor_tensor(T.D[:, 256 * k:256 * k + 256], T.XT[:, 0:4128].indirect(T.XO[:, 16 * k:16 * k + 16]), ap(z), Op.subtract)]
                    add("vector", gx, [v("XT"), v("XO", 16 * k, 16 * k + 16), z], [v("D", 256 * k, 256 * k + 256)], 0.05 + GAT * 256 * CYC)
            tag[0] = "ab"
            act(v("ZW", a, b), v("D", a, b), Act.Abs)
            tag[0] = "bb"
            act(v("BB", a, b), v("D", a, b), Act.Sign, bias=0.5)
            tag[0] = "vi"
            up, V2 = v("pb1", c0, c1), v("pb7", 256 + c0, 256 + c1)
            mms([(up, mat("WRED", lp), v("ZW", a + lp, b, 16), lp == 0, lp == 15) for lp in range(16)])
            V1, UM, V3, V4, V5 = [v(x, c0, c1) for x in ("V1", "UM", "V3", "V4", "V5")]
            cp(V1, up)
            ts(UM, V1, 4095, Op.bitwise_and)
            ts(V2, UM, 1184.0, Op.add)
            tt(V3, UM, V2, Op.mult)
            tt(V4, V3, v("pb2", c0, c1), Op.add)
            ts(V5, V4, 5, Op.arith_shift_right, 4095, Op.bitwise_and)
            cp(v("HO", c0, c1), V5)
            tag[0] = "row"
            if q == 0:
                mms([(v("pb3", 0, 256), v("ZER", 0, 128), v("ZER"), True, False)])
            mms([(v("pb3", c0, c1), mat("RED", lp), v("BB", a + lp, b, 16), False, False) for lp in range(16)])
            if q == 3:
                mms([(v("pb3", 0, 256), v("I32"), v("CM"), False, True)])
                act(v("G1"), v("pb3", 0, 256), Act.Sign, bias=-31.5)
            tag[0] = "pk"
            tt(v("PK", c0, c1), UM, sub(CB, c0, c1), Op.add)
        for q in range(4):
            a, b, c0, c1 = 1024 * q, 1024 * q + 1024, 64 * q, 64 * q + 64
            tag[0] = "vg"

            def gvt(a=a, b=b, c0=c0, c1=c1):
                return [g.vector.tensor_tensor(T.EE[:, a:b], T.VT[:, 0:4096].indirect(T.HO[:, c0:c1]), T.ZW[:, a:b], Op.subtract)]
            add("vector", gvt, [v("VT", 0, 4096), v("HO", c0, c1), v("ZW", a, b)], [v("EE", a, b)], 0.05 + GAT * 1024 * CYC)
            act(v("AB", a, b), v("EE", a, b), Act.Abs)
            tag[0] = "far"
            fp, ff = v("pb4", c0, c1), v("pb7", 256 + c0, 256 + c1)
            ky = ff if q else v("KEY")
            mms([(fp, v("I1K"), v("G1", c0, c1), True, False)] +
                [(fp, mat("RED", lp), v("AB", a + lp, b, 16), False, lp == 15) for lp in range(16)])
            tt(ff, fp, v("TH", c0, c1), Op.is_gt)
            tt(ky, ff, v("PK", c0, c1), Op.mult)
            if q == 0:
                tt(sub(ky, 0, 32), sub(ky, 0, 32), alt, Op.max)
                rm = ky
            else:
                tt(v("RM", c0, c1), rm, ky, Op.max)
                rm = v("RM", c0, c1)
        M1, Wd = L("M1", "LF", 64), L("W", "LI", 64)
        tt(sub(M1, 0, 32), sub(rm, 0, 32), sub(rm, 32, 64), Op.max)
        tt(sub(M1, 32, 64), sub(rm, 0, 32), sub(rm, 32, 64), Op.max)
        tt(sub(Wd, 0, 48), sub(M1, 0, 48), sub(M1, 16, 64), Op.max)
        tt(sub(Wd, 48, 64), sub(M1, 48, 64), sub(M1, 0, 16), Op.max)
        W32 = sub(Wd, 0, 32)
        tag[0] = "mv"
        if not last:
            ts(lane("u" + nxp, "LI", 64), Wd, 4095, Op.bitwise_and)
        za, zb, zo = L("za", "LI", 16), L("zb", "LI", 16), v("ZO", 16 * (s % 2), 16 * (s % 2) + 16)
        ts(za, h16(Wd), 4, Op.arith_shift_right, 0x1F00, Op.bitwise_and)
        tt(zb, za, lc, Op.add)
        cp(zo, zb)
        zn, zw = v("ZW", ZS + 256 * (s + 1), ZS + 256 * (s + 2)), v("ZW", 0, ZS + 256 * (s + 1))

        def gz(zn=zn, zw=zw, zo=zo):
            return [g.scalar.activation(ap(zn), ap(zw).indirect(ap(zo)), Act.Copy)]
        add("scalar", gz, [zw, zo], [zn], 0.065 + GAT * 256 * CYC)
        if last:
            dma("scalar", T.yz[:], ap(zn), [zn], [], "oz", 2.5)
        pop, m = L("pop", "LB"), L("m", "LB")
        tt(pop, W32, kp, Op.is_lt)
        if s and not last:
            cn, ct, am, A = v("pb2", 400, 416), L("ct", "LF", 1), L("am", "LI", 1), L("A", "LF", 1)
            mms([(cn, one, h16(pop), True, True)])
            add("vector", lambda ct=ct, cn=cn: [g.vector.tensor_reduce(ap(ct), ap(cn), AxisListType.X, Op.add)], [cn], [ct], 64 * CYC)
            ts(am, ct, 1.0 / 32, Op.mult, -0.484375, Op.add)
            ts(A, am, -32.0, Op.mult, ct, Op.add)
        tag[0] = "ln"
        tt(m, W32, kth, Op.is_ge)
        hi, y1, y2, tau, y3, dl = L("hi", "LI"), L("y1", "LF"), L("y2", "LF"), L("tau", "LB"), L("y3", "LB"), L("dl", "LB")
        tau4, dl4, pn, pn4 = L("tau4", "LB", 64), L("dl4", "LB", 64), lane("ptr" + nxp, "LB"), L("pn4", "LB", 64)
        ts(hi, W32, 17, Op.arith_shift_right)
        tt(y1, hi, tca, Op.subtract)
        tt(y2, y1, m, Op.mult)
        tt(tau, y2, tca, Op.add)
        tt(y3, m, d2, Op.mult)
        tt(dl, y3, d, Op.subtract)
        for i in range(2):
            act(sub(tau4, 32 * i, 32 * i + 32), tau, Act.Copy)
            act(sub(dl4, 32 * i, 32 * i + 32), dl, Act.Copy)
        mms([(v("pb5", 64 * i, 64 * i + 64), v("IDN"), tau4, True, True) for i in range(4)] +
            [(v("pb5", 256 + 64 * i, 320 + 64 * i), v("IDN"), dl4, True, True) for i in range(4)])
        lv = v("LEV%d" % ((s + 1) % 2))
        tt(v("HIT"), v("CAC"), v("pb5", 0, 256), Op.is_equal)
        tt(v("pb5", 0, 256), v("HIT"), v("pb5", 256, 512), Op.mult)
        tt(lv, v("LEV%d" % (s % 2)), v("pb5", 0, 256), Op.add)
        tt(pn, pop, pt, Op.mult)
        if not last:
            act(sub(pn4, 0, 32), pn, Act.Copy)
            act(sub(pn4, 32, 64), pn, Act.Copy)
            mms([(RTP, v("IDN"), v("RTB"), True, False)] + [(v("pb0", k, 256, 16), v("I64"), sub(lv, 16 * k, 16 * k + 16), False, k == 15) for k in range(16)])
            mms([(CAN, v("IDN"), v("CAB"), True, False), (CAN, v("N64"), lv, False, False)] +
                [(v("pb0", 256 + 64 * i, 320 + 64 * i), v("NEG"), pn4, False, i == 3) for i in range(4)])
            dx, ca_, cb_ = L("dx", "LB"), L("ca_", "LI", 16), L("cb_", "LI", 16)
            tt(dx, d, m, Op.add)
            tt(lane("d" + nxp, "LB"), dx, pop, Op.subtract)
            tt(v("HD", s + 1, 144, NE), h16(m), h16(d1), Op.mult)
            ts(ca_, h16(hi), 4096.0, Op.mult, float((s + 1) * 262144), Op.add)
            tt(cb_, ca_, h16(u), Op.add)
            tt(v("HC", s + 1, 144, NE), cb_, h16(m), Op.mult)
        tag[0] = "dd"
        if s:
            sx, sc = L("sx", "LF", 16), L("sc", "LF", 16)
            act(sx, h16(pop), Act.Identity, scale=-9999.0, bias=9999.0)
            tt(sc, sx, ps, Op.add)
            for lh in range(16):
                ts(v("CMP", 272 * lh, 256 * lh + 256), v("PR", 16 * lh, 256), sub(sc, lh, lh + 1), Op.is_equal)
            mms([(v("pb6", 0, 256), v("IDN"), v("OFFD"), True, False)] +
                [(v("pb6", 16 * lh + 16, 256), v("BLK"), v("CMP", 272 * lh + 16, 256 * lh + 256), False, False) for lh in range(15)] +
                [(v("pb6", lp, 256, 16), mat("TRI", lp), v("CMP", lp, 4096, 272), False, lp == 15) for lp in range(16)])
            scan(v("CS"), v("RSM"), v("pb6", 0, 256), Op.mult, Op.max)
            nc, wn, wa, wb = L("nc", "LF", 16), L("wn", "LF", 16), L("wa", "LF", 16), L("wb", "LF", 16)
            ts(nc, v("CS", 15, 256, 16), 0.5, Op.is_lt)
            tt(wn, nc, h16(pop), Op.mult)
            tt(wa, wn, ad, Op.mult)
            tt(wb, wa, dmp, Op.add)
            cp(wo, wb)
            send(win, wo, "aw%d" % s)
            tag[0] = "sc"

            def scat(lst, src):
                add("vector", lambda: [g.vector.tensor_copy(T.VT[:, 0:4352].indirect(ap(lst)), ap(src))], [lst, src], [v("VT")], 0.05 + 3.8 * 256 * CYC)
            snd = len(ops) - 1
            scat(wo, z)
            ne = len(topo.engines(prv, core)[:8])
            add("net", None, [], [win, zin], 3.0, [("az%d" % s, ne), ("aw%d" % s, ne)], [snd])
            scat(win, zin)
    tag[0] = "out"
    dma("sync", T.yv[:], T.VT[:, 0:4096], [v("VT")], [], "ov", 8.0)
    pz = h16(lane("ptr_0", "LB"))
    add("tensor", lambda: [g.tensor.matmul(T.pb1[0:8, lp:256:16], T.BSEL[:, lp * 128:lp * 128 + 128:16], ap(pz), True, True) for lp in range(16)],
        [v("BSEL"), pz], [v("pb1", 0, 256)], 1.0)
    add("vector", lambda: [g.vector.tensor_scalar(T.YP[0:8, :], T.pb1[0:8, 0:256], -1.0, None, Op.add)], [v("pb1", 0, 256)], [v("YP")], 0.22)
    dma("sync", T.yp[:], T.YP[0:8, :], [v("YP")], [], "op", 2.5)
    mms([(v("pb0", k, 256, 16), v("IDN"), sub(lv, 16 * k, 16 * k + 16), True, True) for k in range(16)])
    cp(v("LEV"), RTP)
    mms([(v("pb3", 32 * b + 16 * gp, 32 * b + 16 * gp + 16), smx(lhp, gp), v("LEV", (2 * b + lhp) * 16, (2 * b + lhp) * 16 + 16), lhp == 0, lhp == 1)
         for b in range(8) for gp in range(2) for lhp in range(2)])
    cp(v("LVT"), v("pb3", 0, 256))
    turn(v("YL"), v("LVT"))
    cp(v("YLB"), v("YL"))
    dma("scalar", T.yl[:], T.YLB[:], [v("YLB")], [], "ol", 2.5)
    queues = {"vector": g.vector, "scalar": g.scalar, "tensor": g.tensor, "gpsimd": g, "sync": g.sync}
    schedule(g, T, ops, queues)
    g.wait_ge(T.sem.loc, 2 * (STEPS - 1) * len(topo.engines(core, nxt)[:8]))


def schedule(g, T, ops, queues):
    N = len(ops)
    preds = [dict() for _ in range(N)]
    hist = {}
    for i, o in enumerate(ops):
        for p in o["pre"]:
            preds[i][p] = o["q"] != "net"
        for kind, regs in (("r", o["rd"]), ("w", o["wr"])):
            for (name, c0, c1, st) in regs:
                ps = SCRATCH[name][0] == "psum"
                for (j, k2, b0, b1) in hist.get(name, ()):
                    if j == i:
                        continue
                    same = ops[j]["q"] == o["q"] and not ops[j]["done"]
                    if b0 < c1 and c0 < b1 and (kind == "w" or k2 == "w"):
                        need = (not same) or k2 == "w"
                        if same and o["q"] == "tensor" and ps:
                            need = False
                        preds[i][j] = preds[i].get(j, False) or need
                    elif ps and not same:
                        preds[i][j] = True
        for kind, regs in (("r", o["rd"]), ("w", o["wr"])):
            for (name, c0, c1, st) in regs:
                h = hist.setdefault(name, [])
                if kind == "w" and st == 1:
                    keep = SCRATCH[name][0] == "psum"
                    h[:] = [x for x in h if not (c0 <= x[2] and x[3] <= c1 and x[0] != i) or (keep and x[0] > i - 600)]
                h.append((i, kind, c0, c1))
    succ = [[] for _ in range(N)]
    for i in range(N):
        for j in preds[i]:
            succ[j].append(i)
    prio = [0.0] * N
    for i in range(N - 1, -1, -1):
        prio[i] = ops[i]["cost"] + max([prio[x] + LAT for x in succ[i]] + [0.0])
    own = [prio[i] + BIAS.get(ops[i]["tag"], 0.0) for i in range(N)]
    left = [len(p) for p in preds]
    est, end = [0.0] * N, [0.0] * N
    free, ready, order, seq = {}, {}, {}, []
    for i in range(N):
        if not left[i]:
            ready.setdefault(ops[i]["q"], []).append(i)
    for _ in range(N):
        best = None
        for q, lst in ready.items():
            if not lst:
                continue
            f = free.get(q, 0.0)
            t0 = min(max(f, est[i]) for i in lst)
            i = max((x for x in lst if max(f, est[x]) <= t0 + WIN), key=lambda x: own[x])
            t = max(f, est[i])
            if best is None or t < best[0]:
                best = (t, q, i)
        t, q, i = best
        ready[q].remove(i)
        end[i] = t + ops[i]["cost"]
        free[q] = t if q == "net" else t + 0.1 if ops[i]["done"] and ops[i]["done"][1] else end[i]
        order.setdefault(q, []).append(i)
        seq.append(i)
        for x in succ[i]:
            est[x] = max(est[x], t if ops[x]["q"] == q and not preds[x][i] else end[i] + LAT)
            left[x] -= 1
            if not left[x]:
                ready.setdefault(ops[x]["q"], []).append(x)
    count = {q: 0 for q in QSEM}
    known, fin = {}, [None] * N
    for i in seq:
        o = ops[i]
        q = o["q"]
        if q == "net":
            fin[i] = (list(o["done"]), {})
            continue
        kq = known.setdefault(q, {})
        pj = [j for j, c in preds[i].items() if c]
        need = {}
        for j in pj:
            for sem, val in fin[j][0]:
                if sem != "none" and kq.get(sem, 0) < val:
                    need[sem] = max(need.get(sem, 0), val)
        for j in pj:
            for sem, val in fin[j][1].items():
                if sem in need and need[sem] <= val and sem not in [x[0] for x in fin[j][0]]:
                    del need[sem]
        for sem, val in sorted(need.items()):
            queues[q].wait_ge(T.sem[sem], val)
            kq[sem] = max(kq.get(sem, 0), val)
        for j in pj:
            for sem, val in list(fin[j][1].items()) + fin[j][0]:
                kq[sem] = max(kq.get(sem, 0), val)
        ins = o["fn"]()
        if o["done"]:
            sem, val = o["done"]
            for x in ins:
                x.then_inc(T.sem[sem], val)
            fin[i] = ([(sem, val)], dict(kq))
        else:
            for x in ins:
                x.then_inc(T.sem[QSEM[q]], 1)
            count[q] += len(ins)
            fin[i] = ([(QSEM[q], count[q])], dict(kq))
    for q in QSEM:
        if count[q]:
            g.wait_ge(T.sem[QSEM[q]], count[q])
    for sem in LOADS + OUTS:
        g.wait_ge(T.sem[sem], 16)
    return max(end), order, end
